import numpy as np
import ml_dtypes


def mxq(x, axis, fmt="e4m3"):
    dtype, down = {"e4m3": (ml_dtypes.float8_e4m3fn, 7), "e5m2": (ml_dtypes.float8_e5m2, 14)}[fmt]
    v = np.moveaxis(np.asarray(x, np.float32).astype(ml_dtypes.bfloat16).astype(np.float64), axis, -1)
    blocks = v.reshape(v.shape[:-1] + (-1, 32))
    amax = np.abs(blocks).max(-1, keepdims=True)
    byte = np.maximum(np.where(amax > 0, np.frexp(amax)[1] - 1 + 127, 0) - down, 1)
    scale = np.exp2(byte - 127.0)
    codes = (blocks / scale).astype(np.float32).astype(dtype).astype(np.float64)
    return np.moveaxis((codes * scale).reshape(v.shape), -1, axis)


WIDE = False


def mx_kscale(k):
    if not WIDE:
        return np.ones(k)
    levels = np.array([10, -10, 5, -5, 0])
    if k % 512:
        return np.exp2(np.random.permutation(np.resize(levels, k // 32))).repeat(32)
    a = np.empty((k // 512, 16))
    for p in range(k // 512):
        a[p, :8] = np.random.permutation(np.resize(levels, 8))
        for g in range(8):
            far = levels[np.abs(levels - a[p, g]) >= 10]
            a[p, g + 8] = far[np.random.randint(len(far))]
    return np.exp2(a.ravel()).repeat(32)


def f64(x):
    return np.asarray(x).astype(np.float64)


def striped(idx):
    return np.tile(np.asarray(idx).reshape(-1, 16).T, (8, 1)).astype(np.uint16)


def unstriped(offs):
    return offs[:16].T.reshape(-1).astype(np.int64)


E2M1 = np.array([0.0, 0.5, 1.0, 1.5, 2.0, 3.0, 4.0, 6.0, -0.0, -0.5, -1.0, -1.5, -2.0, -3.0, -4.0, -6.0])


def pack_weight(w, fmt):
    k, n = w.shape
    w = f64(np.asarray(w, np.float32).astype(ml_dtypes.bfloat16)).reshape(k // 32, 32, n)
    amax = np.abs(w).max(1)
    if fmt == "e4m3":
        byte = np.frexp(amax)[1] - 1 + 127 - 7
    else:
        mant, ex = np.frexp(amax / 6.0)
        byte = np.where(mant > 0.5, ex, ex - 1) + 127
    byte = np.clip(np.where(amax > 0, byte, 1), 1, 254)
    scaled = (w * np.exp2(127.0 - byte)[:, None, :]).reshape(k, n).astype(np.float32)
    by_word = np.ascontiguousarray(scaled.reshape(k // 512, 128, 4, n).transpose(0, 1, 3, 2))
    if fmt == "e4m3":
        words = by_word.astype(ml_dtypes.float8_e4m3fn).view(np.uint8)
    else:
        c = by_word.astype(ml_dtypes.float4_e2m1fn).view(np.uint8) & 0xF
        words = (c[..., 0::2] | (c[..., 1::2] << 4)).reshape(k // 512, 128, 2 * n)
    return np.ascontiguousarray(words), np.ascontiguousarray(byte.astype(np.uint8).reshape(k // 512, 16, n))


def unpack_weight(words, scales, fmt):
    g, _, n = scales.shape
    words = np.ascontiguousarray(words).reshape(g, 128, n, -1)
    if fmt == "e4m3":
        vals = words.view(ml_dtypes.float8_e4m3fn).astype(np.float64)
    else:
        nib = np.empty((g, 128, n, 4), np.uint8)
        nib[..., 0::2] = words & 0xF
        nib[..., 1::2] = words >> 4
        vals = E2M1[nib]
    vals = vals * np.repeat(np.exp2(scales.astype(np.float64) - 127.0), 8, axis=1)[..., None]
    return vals.transpose(0, 1, 3, 2).reshape(g * 512, n)


def sigmoid(v):
    return 1.0 / (1.0 + np.exp(-v))


D, T, I, Q, E, U, Z, M, C = 512, 2048, 512, 256, 512, 1024, 1024, 1024, 512


def setup_inputs():
    n = np.random.standard_normal
    idx = np.random.permutation(T)[:I]
    idx2 = np.random.permutation(U)[:I]
    idx3 = np.random.permutation(Z)[:I]
    idx4 = np.random.permutation(M)[:Q]
    fd = mx_kscale(D)
    fi = mx_kscale(I)
    fc = mx_kscale(C)
    ti = np.ones(T)
    ti[idx] = fi
    keysp = pack_weight(n((D, T)) / fd[:, None], "e4m3")
    return {
        "query": (n((D, Q)) * 0.6 / np.sqrt(D) * fd[:, None]).astype(np.float32),
        "query2": (n((D, Q)) * 0.6 / np.sqrt(D) * fd[:, None]).astype(np.float32),
        "query3": (n((D, Q)) * 0.6 / np.sqrt(D) * fd[:, None]).astype(np.float32),
        "keys_words": keysp[0],
        "keys_scales": keysp[1],
        "notes": (n((D, U)) / fd[:, None]).astype(np.float32),
        "pages": (n((D, Z)) / fd[:, None]).astype(np.float32),
        "os": (np.random.uniform(0.02, 0.08, (1, I)) * fi).astype(np.float32),
        "vals": (n((E, T)) / ti).astype(np.float32),
        "wm": (n((C, E)) * 1.0 / np.sqrt(C) * fc[:, None]).astype(np.float32),
        "mstore": (n((C, M)) / fc[:, None]).astype(np.float32),
        "offs": striped(idx),
        "offs2": striped(idx2),
        "offs3": striped(idx3),
        "offs4": striped(idx4),
    }


def reference(query, query2, query3, keys_words, keys_scales, notes, pages, os, vals, wm, mstore, offs, offs2, offs3, offs4):
    idx = unstriped(offs)
    idx2 = unstriped(offs2)
    idx3 = unstriped(offs3)
    idx4 = unstriped(offs4)
    keysu = unpack_weight(keys_words, keys_scales, "e4m3")
    queryq = mxq(f64(query), 0, "e4m3")
    keysidxg = keysu[:, idx]
    query2q = mxq(f64(query2), 0, "e4m3")
    notesidx2q = mxq(f64(notes)[:, idx2], 0, "e4m3")
    query3q = mxq(f64(query3), 0, "e4m3")
    pagesidx3q = mxq(f64(pages)[:, idx3], 0, "e4m3")
    s = queryq.T @ keysidxg + query2q.T @ notesidx2q + query3q.T @ pagesidx3q
    w = sigmoid(s)
    wo1 = w * f64(os)
    wt1 = wo1.T
    vt1 = f64(vals)[:, idx].T
    vt1q = mxq(vt1, 0, "e4m3")
    wt1q = mxq(wt1, 0, "e4m3")
    o = vt1q.T @ wt1q
    wmq = mxq(f64(wm), 0, "e4m3")
    mstoreq = mxq(f64(mstore), 0, "e4m3")
    me = wmq.T @ mstoreq
    y = np.maximum(o, me[:, idx4])
    return y

@@ -1,0 +1,211 @@
+from contextlib import ExitStack
+
+import concourse.mybir as mybir
+from concourse.masks import make_identity
+
+D, T, I, Q, E, U, M, C = 512, 2048, 512, 256, 512, 1024, 1024, 512
+FLOPS = 2 * (3 * D * Q * I + I * E * Q + C * E * M)
+
+F32 = mybir.dt.float32
+BF16 = mybir.dt.bfloat16
+I32 = mybir.dt.int32
+U32 = mybir.dt.uint32
+U16 = mybir.dt.uint16
+U8 = mybir.dt.uint8
+FP8X4 = mybir.dt.float8_e4m3fn_x4
+COPY = mybir.ActivationFunctionType.Copy
+SIGMOID = mybir.ActivationFunctionType.Sigmoid
+MULT = mybir.AluOpType.mult
+MAX = mybir.AluOpType.max
+
+P = 128
+PACK = 4
+BANK = 512
+GROUP = 16
+
+
+def weave(copy, dst, src):
+    copy(dst.rearrange("p (c i) t -> p c t i", i=4), src.rearrange("p t (c i) -> p c t i", i=4))
+
+
+def tile_attend_threesources_memorylarger_lean_kernel(
+    tc, query, query2, query3, keys_words, keys_scales, notes, pages, slot_factor, vals, wm, mstore,
+    offs, offs2, offs3, offs4, out,
+):
+    nc = tc.nc
+    with ExitStack() as ctx:
+        lists = ctx.enter_context(tc.tile_pool(name="lists", bufs=1))
+        sb = ctx.enter_context(tc.tile_pool(name="sb", bufs=1))
+        ps = ctx.enter_context(tc.psum_pool(name="ps", bufs=1))
+
+        def buffer(name, shape, dtype, reuse=None):
+            return sb.tile(shape, dtype, name=name, tag=reuse or name, align_bytes=64)
+
+        def quantize(name, woven, width, reuse=None):
+            codes = buffer(name + "_codes", [P, width], U32, reuse)
+            scales = buffer(name + "_scales", [P, width], U8)
+            nc.vector.quantize_mx(codes[:].bitcast(FP8X4), scales[:], woven.rearrange("p w t -> p (w t)"))
+            return codes, scales
+
+        def mx(acc, left, cols, right, start, stop):
+            nc.tensor.matmul_mx(
+                acc, lhsT=left[0][:, cols].bitcast(FP8X4), lhsT_scale=left[1][:, cols],
+                rhs=right[0][:].bitcast(FP8X4), rhs_scale=right[1][:], start=start, stop=stop,
+            )
+
+        def load_rows(name, src):
+            raw = buffer(name, [P, PACK, src.shape[1]], F32)
+            nc.sync.dma_start(raw[:], src.rearrange("(p t) w -> p t w", t=PACK))
+            return raw
+
+        def load_planes(name, src):
+            planes = []
+            for t in range(PACK):
+                plane = buffer(name + str(t), [P, src.shape[1]], F32)
+                nc.sync.dma_start(plane[:], src.rearrange("(p t) w -> p t w", t=PACK)[:, t, :])
+                planes.append(plane)
+            return planes
+
+        def load_list(name, src):
+            tile = lists.tile([P, src.shape[1]], U16, name=name)
+            nc.sync.dma_start(tile[:], src)
+            return tile
+
+        def scalar_gather(dst, src):
+            nc.scalar.activation(dst, src, COPY)
+
+        key_scales = buffer("key_scales", [P, T], U8)
+        nc.vector.memset(key_scales[:].bitcast(I32), 0)
+        for quad in range(4):
+            nc.gpsimd.dma_start(
+                key_scales[32 * quad : 32 * quad + 4, :].bitcast(I32),
+                keys_scales[0, 4 * quad : 4 * quad + 4, :].bitcast(I32),
+            )
+        factor = buffer("factor", [P, PACK], F32)
+        nc.gpsimd.dma_start(factor[:], slot_factor.rearrange("o (p t) -> (o p) t", t=PACK))
+        ident = buffer("ident", [P, P], F32)
+        make_identity(nc, ident[:])
+
+        wm_raw = load_rows("wm_raw", wm)
+        token_list = load_list("token_list", offs)
+        note_list = load_list("note_list", offs2)
+        page_list = load_list("page_list", offs3)
+        memory_list = load_list("memory_list", offs4)
+        ms_raw = [load_rows("ms_raw" + str(h), mstore[:, h * BANK : (h + 1) * BANK]) for h in range(M // BANK)]
+        note_planes = load_planes("note_plane", notes)
+        key_words = buffer("key_words", [P, T], I32)
+        nc.sync.dma_start(key_words[:], keys_words[0].rearrange("p n t -> p (n t)").bitcast(I32))
+        page_planes = load_planes("page_plane", pages)
+        q_raw = [load_rows("q_raw" + str(n), src) for n, src in enumerate((query2, query, query3))]
+        val_rows = []
+        for a in range(E // P):
+            rows = buffer("val_rows" + str(a), [P, T], F32)
+            nc.sync.dma_start(rows[:], vals[a * P : (a + 1) * P, :])
+            val_rows.append(rows)
+
+        wm_woven = buffer("wm_woven", [P, E, PACK], BF16)
+        weave(nc.vector.tensor_copy, wm_woven[:], wm_raw[:])
+        wm_q = quantize("wm", wm_woven[:], E)
+        memories = [buffer("memories" + str(a), [P, M], F32) for a in range(E // P)]
+        for half in range(M // BANK):
+            woven = buffer("ms_woven" + str(half), [P, BANK, PACK], BF16)
+            weave(nc.vector.tensor_copy, woven[:], ms_raw[half][:])
+            ms_q = quantize("ms" + str(half), woven[:], BANK)
+            for a in range(E // P):
+                acc = ps.tile([P, BANK], F32, name="me_acc", tag="acc", bufs=4)
+                mx(acc[:], wm_q, slice(a * P, (a + 1) * P), ms_q, True, True)
+                nc.scalar.copy(memories[a][:, half * BANK : (half + 1) * BANK], acc[:])
+
+        note_picked = buffer("note_picked", [P, PACK, I], BF16)
+        for t in range(PACK):
+            gather = nc.vector.tensor_copy if t < PACK - 1 else scalar_gather
+            gather(note_picked[:, t, :], note_planes[t][:].indirect(note_list[:]))
+
+        def weave_quantize(name, picked, reuse):
+            woven = buffer(name + "_woven", [P, I, PACK], BF16, reuse)
+            weave(nc.vector.tensor_copy, woven[:], picked[:])
+            return quantize(name, woven[:], I)
+
+        def look_up(a, gather, reuse):
+            picked = buffer("picked_memories" + str(a), [P, Q], F32, reuse)
+            gather(picked[:], memories[a][:].indirect(memory_list[:]))
+            return picked
+
+        note_q = weave_quantize("note", note_picked, None)
+        picked_words = buffer("picked_words", [P, I], U32, "note_picked")
+        nc.vector.tensor_copy(picked_words[:], key_words[:].bitcast(U32).indirect(token_list[:]))
+        picked_scales = buffer("picked_scales", [P, I], U8, "key_words")
+        nc.vector.tensor_copy(picked_scales[:], key_scales[:].indirect(token_list[:]))
+        key_q = (picked_words, picked_scales)
+        picked_memories = [
+            look_up(a, scalar_gather, reuse) for a, reuse in enumerate(("note_plane3", "memories0", "memories1"))
+        ]
+
+
+        def gather_in_halves(dst, window, offsets):
+            cols = I // 2 // GROUP
+            scalar_gather(dst[:, : I // 2], window.indirect(offsets[:, :cols]))
+            nc.vector.tensor_copy(dst[:, I // 2 :], window.indirect(offsets[:, cols:]))
+
+        page_picked = buffer("page_picked", [P, PACK, I], BF16)
+        for t in range(PACK - 1):
+            scalar_gather(page_picked[:, t, :], page_planes[t][:].indirect(page_list[:]))
+        gather_in_halves(page_picked[:, PACK - 1, :], page_planes[PACK - 1][:], page_list)
+        page_q = weave_quantize("page", page_picked, None)
+
+        q_q = []
+        for n, copy in enumerate((nc.scalar.copy, nc.scalar.copy, nc.vector.tensor_copy)):
+            woven = buffer("q_woven" + str(n), [P, Q, PACK], BF16)
+            weave(copy, woven[:], q_raw[n][:])
+            q_q.append(quantize("q" + str(n), woven[:], Q))
+
+        scores = [ps.tile([P, I], F32, name="scores" + str(h), tag="score", bufs=2) for h in range(Q // P)]
+        for n, keys in enumerate((note_q, key_q, page_q)):
+            for h in range(Q // P):
+                mx(scores[h][:], q_q[n], slice(h * P, (h + 1) * P), keys, n == 0, n == 2)
+        sig = []
+        for h in range(Q // P):
+            dealt = buffer("sig" + str(h), [P, PACK, P], F32)
+            nc.scalar.activation(dealt[:], scores[h][:].rearrange("p (s t) -> p t s", t=PACK), SIGMOID)
+            sig.append(dealt)
+        picked_memories.append(look_up(3, scalar_gather, "q2_codes"))
+        picked_first = buffer("picked_vals0", [P, I], BF16, "q_woven2")
+        nc.vector.tensor_copy(picked_first[:], val_rows[0][:].indirect(token_list[:]))
+        w_woven = buffer("w_woven", [P, Q, PACK], BF16, "val_rows0")
+        for h in range(Q // P):
+            turned = ps.tile([P, PACK, P], F32, name="w_turned", tag="score", bufs=2)
+            for t in range(PACK):
+                nc.tensor.transpose(turned[:, t, :], sig[h][:, t, :], ident[:])
+            nc.vector.tensor_tensor(
+                w_woven[:, h * P : (h + 1) * P, :], turned[:].rearrange("p t q -> p q t"),
+                factor[:].unsqueeze(1).to_broadcast([P, P, PACK]), MULT,
+            )
+        w_q = quantize("w", w_woven[:], Q)
+
+        def value_block(a, picked, bank, reuse):
+            words = picked[:].bitcast(F32)
+            turned = ps.tile([P, 2, P], F32, name="v_turned", tag=bank)
+            for u in range(2):
+                nc.tensor.transpose(turned[:, u, :], words[:, u::2], ident[:])
+            woven = buffer("v_woven" + str(a), [P, P, PACK], BF16, reuse)
+            nc.scalar.copy(woven[:].bitcast(F32), turned[:].rearrange("p u e -> p e u"))
+            return quantize("v" + str(a), woven[:], P)
+
+        def finish(a, v_q, acc, reuse):
+            mx(acc[:], v_q, slice(0, P), w_q, True, True)
+            result = buffer("result" + str(a), [P, Q], F32, reuse)
+            nc.vector.tensor_tensor(result[:], acc[:], picked_memories[a][:], MAX)
+            nc.sync.dma_start(out[a * P : (a + 1) * P, :], result[:])
+
+        picked_vals = [picked_first] + [buffer("picked_vals" + str(a), [P, I], BF16) for a in (1, 2, 3)]
+        scalar_gather(picked_vals[1][:], val_rows[1][:].indirect(token_list[:]))
+        v0 = value_block(0, picked_vals[0], "turn_a", "val_rows1")
+        v1 = value_block(1, picked_vals[1], "turn_b", None)
+        gather_in_halves(picked_vals[2][:], val_rows[2][:], token_list)
+        v2 = value_block(2, picked_vals[2], "turn_a", None)
+        finish(0, v0, ps.tile([P, Q], F32, name="o0", tag="turn_b"), "val_rows2")
+        gather_in_halves(picked_vals[3][:], val_rows[3][:], token_list)
+        v3 = value_block(3, picked_vals[3], "turn_a", None)
+        finish(1, v1, ps.tile([P, Q], F32, name="o1", tag="acc", bufs=4), "val_rows3")
+        finish(2, v2, ps.tile([P, Q], F32, name="o2", tag="acc", bufs=4), "picked_vals3")
+        finish(3, v3, ps.tile([P, Q], F32, name="o3", tag="acc", bufs=4), None)

@@ -126,20 +126,18 @@ def tile_attend_threesources_memorylarger_lean_kernel(
             weave(nc.vector.tensor_copy, woven[:], picked[:])
             return quantize(name, woven[:], I)
 
-        def look_up(a, gather, reuse):
-            picked = buffer("picked_memories" + str(a), [P, Q], F32, reuse)
-            gather(picked[:], memories[a][:].indirect(memory_list[:]))
+        def look_up(first, gather, reuse):
+            picked = buffer("picked_memories" + str(first), [P, 2, Q], F32, reuse)
+            for a in range(2):
+                gather(picked[:, a, :], memories[first + a][:].indirect(memory_list[:]))
             return picked
 
-        note_q = weave_quantize("note", note_picked, None)
-        picked_words = buffer("picked_words", [P, I], U32, "note_picked")
+        picked_words = buffer("picked_words", [P, I], U32)
         nc.vector.tensor_copy(picked_words[:], key_words[:].bitcast(U32).indirect(token_list[:]))
+        note_q = weave_quantize("note", note_picked, "key_words")
         picked_scales = buffer("picked_scales", [P, I], U8, "key_words")
         nc.vector.tensor_copy(picked_scales[:], key_scales[:].indirect(token_list[:]))
         key_q = (picked_words, picked_scales)
-        picked_memories = [
-            look_up(a, scalar_gather, reuse) for a, reuse in enumerate(("note_plane3", "memories0", "memories1"))
-        ]
 
 
         def gather_in_halves(dst, window, offsets):
@@ -159,6 +157,8 @@ def tile_attend_threesources_memorylarger_lean_kernel(
             weave(copy, woven[:], q_raw[n][:])
             q_q.append(quantize("q" + str(n), woven[:], Q))
 
+        low_memories = look_up(0, scalar_gather, "q_raw1")
+
         scores = [ps.tile([P, I], F32, name="scores" + str(h), tag="score", bufs=2) for h in range(Q // P)]
         for n, keys in enumerate((note_q, key_q, page_q)):
             for h in range(Q // P):
@@ -168,10 +168,21 @@ def tile_attend_threesources_memorylarger_lean_kernel(
             dealt = buffer("sig" + str(h), [P, PACK, P], F32)
             nc.scalar.activation(dealt[:], scores[h][:].rearrange("p (s t) -> p t s", t=PACK), SIGMOID)
             sig.append(dealt)
-        picked_memories.append(look_up(3, scalar_gather, "q2_codes"))
-        picked_first = buffer("picked_vals0", [P, I], BF16, "q_woven2")
-        nc.vector.tensor_copy(picked_first[:], val_rows[0][:].indirect(token_list[:]))
-        w_woven = buffer("w_woven", [P, Q, PACK], BF16, "val_rows0")
+
+        def turn(bank, picked):
+            words = picked[:].bitcast(F32)
+            for u in range(2):
+                nc.tensor.transpose(bank[:, u, :], words[:, u::2], ident[:])
+
+        picked_vals = [
+            buffer("picked_vals" + str(a), [P, I], BF16, reuse)
+            for a, reuse in enumerate(("q_woven2", "q2_codes", None, None))
+        ]
+        low_turned = ps.tile([P, 2, 2, P], F32, name="low_turned", tag="turn_a")
+        nc.vector.tensor_copy(picked_vals[0][:], val_rows[0][:].indirect(token_list[:]))
+        turn(low_turned[:, 0], picked_vals[0])
+        high_memories = look_up(2, nc.vector.tensor_copy, "val_rows0")
+        w_woven = buffer("w_woven", [P, Q, PACK], BF16, "memories3")
         for h in range(Q // P):
             turned = ps.tile([P, PACK, P], F32, name="w_turned", tag="score", bufs=2)
             for t in range(PACK):
@@ -182,30 +193,40 @@ def tile_attend_threesources_memorylarger_lean_kernel(
             )
         w_q = quantize("w", w_woven[:], Q)
 
-        def value_block(a, picked, bank, reuse):
-            words = picked[:].bitcast(F32)
-            turned = ps.tile([P, 2, P], F32, name="v_turned", tag=bank)
-            for u in range(2):
-                nc.tensor.transpose(turned[:, u, :], words[:, u::2], ident[:])
-            woven = buffer("v_woven" + str(a), [P, P, PACK], BF16, reuse)
-            nc.scalar.copy(woven[:].bitcast(F32), turned[:].rearrange("p u e -> p e u"))
-            return quantize("v" + str(a), woven[:], P)
-
-        def finish(a, v_q, acc, reuse):
-            mx(acc[:], v_q, slice(0, P), w_q, True, True)
-            result = buffer("result" + str(a), [P, Q], F32, reuse)
-            nc.vector.tensor_tensor(result[:], acc[:], picked_memories[a][:], MAX)
-            nc.sync.dma_start(out[a * P : (a + 1) * P, :], result[:])
-
-        picked_vals = [picked_first] + [buffer("picked_vals" + str(a), [P, I], BF16) for a in (1, 2, 3)]
         scalar_gather(picked_vals[1][:], val_rows[1][:].indirect(token_list[:]))
-        v0 = value_block(0, picked_vals[0], "turn_a", "val_rows1")
-        v1 = value_block(1, picked_vals[1], "turn_b", None)
-        gather_in_halves(picked_vals[2][:], val_rows[2][:], token_list)
-        v2 = value_block(2, picked_vals[2], "turn_a", None)
-        finish(0, v0, ps.tile([P, Q], F32, name="o0", tag="turn_b"), "val_rows2")
+        turn(low_turned[:, 1], picked_vals[1])
+        scalar_gather(picked_vals[2][:], val_rows[2][:].indirect(token_list[:]))
+        turned2 = ps.tile([P, 2, P], F32, name="turned2", tag="turn_b")
+        turn(turned2, picked_vals[2])
+
+        low_woven = buffer("low_woven", [P, 2 * P, PACK], BF16, "val_rows2")
+        nc.scalar.copy(
+            low_woven[:].bitcast(F32).rearrange("p (a e) u -> p a e u", a=2),
+            low_turned[:].rearrange("p a u e -> p a e u"),
+        )
+        low_q = quantize("low_vals", low_woven[:], 2 * P)
+        low_acc = ps.tile([P, 2, Q], F32, name="low_acc", tag="acc", bufs=4)
+        for a in range(2):
+            mx(low_acc[:, a, :], low_q, slice(a * P, (a + 1) * P), w_q, True, True)
+
         gather_in_halves(picked_vals[3][:], val_rows[3][:], token_list)
-        v3 = value_block(3, picked_vals[3], "turn_a", None)
-        finish(1, v1, ps.tile([P, Q], F32, name="o1", tag="acc", bufs=4), "val_rows3")
-        finish(2, v2, ps.tile([P, Q], F32, name="o2", tag="acc", bufs=4), "picked_vals3")
-        finish(3, v3, ps.tile([P, Q], F32, name="o3", tag="acc", bufs=4), None)
+        turned3 = ps.tile([P, 2, P], F32, name="turned3", tag="turn_a")
+        turn(turned3, picked_vals[3])
+
+        def multiply(a, turned, copy, reuse):
+            woven = buffer("v_woven" + str(a), [P, P, PACK], BF16, reuse)
+            copy(woven[:].bitcast(F32), turned[:].rearrange("p u e -> p e u"))
+            v_q = quantize("v" + str(a), woven[:], P)
+            acc = ps.tile([P, Q], F32, name="high_acc", tag="acc", bufs=4)
+            mx(acc[:], v_q, slice(0, P), w_q, True, True)
+            return acc
+
+        acc2 = multiply(2, turned2, nc.vector.tensor_copy, "val_rows3")
+        low_result = buffer("low_result", [P, 2, Q], F32, "val_rows3")
+        nc.vector.tensor_tensor(low_result[:], low_acc[:], low_memories[:], MAX)
+        nc.sync.dma_start(out[: 2 * P, :].rearrange("(a p) q -> p a q", a=2), low_result[:])
+        acc3 = multiply(3, turned3, nc.scalar.copy, None)
+        for a, acc in ((2, acc2), (3, acc3)):
+            result = buffer("result" + str(a), [P, Q], F32)
+            nc.vector.tensor_tensor(result[:], acc[:], high_memories[:, a - 2, :], MAX)
+            nc.sync.dma_start(out[a * P : (a + 1) * P, :], result[:])

@@ -60,10 +60,10 @@ def tile_attend_threesources_memorylarger_lean_kernel(
 
         def load_planes(name, src):
             planes = []
-            for t in range(PACK):
-                plane = buffer(name + str(t), [P, src.shape[1]], F32)
-                nc.sync.dma_start(plane[:], src.rearrange("(p t) w -> p t w", t=PACK)[:, t, :])
-                planes.append(plane)
+            for pair in range(PACK // 2):
+                both = buffer(name + str(pair), [P, 2, src.shape[1]], F32)
+                nc.sync.dma_start(both[:], src.rearrange("(p t) w -> p t w", t=PACK)[:, 2 * pair : 2 * pair + 2, :])
+                planes.extend([both[:, 0, :], both[:, 1, :]])
             return planes
 
         def load_list(name, src):
@@ -76,13 +76,6 @@ def tile_attend_threesources_memorylarger_lean_kernel(
 
         key_scales = buffer("key_scales", [P, T], U8)
         nc.vector.memset(key_scales[:].bitcast(I32), 0)
-        for quad in range(4):
-            nc.gpsimd.dma_start(
-                key_scales[32 * quad : 32 * quad + 4, :].bitcast(I32),
-                keys_scales[0, 4 * quad : 4 * quad + 4, :].bitcast(I32),
-            )
-        factor = buffer("factor", [P, PACK], F32)
-        nc.gpsimd.dma_start(factor[:], slot_factor.rearrange("o (p t) -> (o p) t", t=PACK))
         ident = buffer("ident", [P, P], F32)
         make_identity(nc, ident[:])
 
@@ -91,11 +84,18 @@ def tile_attend_threesources_memorylarger_lean_kernel(
         note_list = load_list("note_list", offs2)
         page_list = load_list("page_list", offs3)
         memory_list = load_list("memory_list", offs4)
-        ms_raw = [load_rows("ms_raw" + str(h), mstore[:, h * BANK : (h + 1) * BANK]) for h in range(M // BANK)]
+        ms_raw = load_rows("ms_raw", mstore)
         note_planes = load_planes("note_plane", notes)
         key_words = buffer("key_words", [P, T], I32)
         nc.sync.dma_start(key_words[:], keys_words[0].rearrange("p n t -> p (n t)").bitcast(I32))
+        for quad in range(4):
+            nc.sync.dma_start(
+                key_scales[32 * quad : 32 * quad + 4, :].bitcast(I32),
+                keys_scales[0, 4 * quad : 4 * quad + 4, :].bitcast(I32),
+            )
         page_planes = load_planes("page_plane", pages)
+        factor = buffer("factor", [P, PACK], F32)
+        nc.sync.dma_start(factor[:], slot_factor.rearrange("o (p t) -> (o p) t", t=PACK))
         q_raw = [load_rows("q_raw" + str(n), src) for n, src in enumerate((query2, query, query3))]
         val_rows = []
         for a in range(E // P):
@@ -106,25 +106,23 @@ def tile_attend_threesources_memorylarger_lean_kernel(
         wm_woven = buffer("wm_woven", [P, E, PACK], BF16)
         weave(nc.vector.tensor_copy, wm_woven[:], wm_raw[:])
         wm_q = quantize("wm", wm_woven[:], E)
+
+        def gather_plane(picked, planes, offsets, t, gather):
+            gather(picked[:, t, :], planes[t].indirect(offsets[:]))
+
+        vector_gather = nc.vector.tensor_copy
+        ms_woven = [buffer("ms_woven" + str(half), [P, BANK, PACK], BF16) for half in range(M // BANK)]
+        for half, copy in enumerate((nc.vector.tensor_copy, nc.scalar.copy)):
+            weave(copy, ms_woven[half][:], ms_raw[:, :, half * BANK : (half + 1) * BANK])
+        note_picked = buffer("note_picked", [P, PACK, I], F32)
+        gather_plane(note_picked, note_planes, note_list, 0, scalar_gather)
         memories = [buffer("memories" + str(a), [P, M], F32) for a in range(E // P)]
         for half in range(M // BANK):
-            woven = buffer("ms_woven" + str(half), [P, BANK, PACK], BF16)
-            weave(nc.vector.tensor_copy, woven[:], ms_raw[half][:])
-            ms_q = quantize("ms" + str(half), woven[:], BANK)
+            ms_q = quantize("ms" + str(half), ms_woven[half][:], BANK)
             for a in range(E // P):
                 acc = ps.tile([P, BANK], F32, name="me_acc", tag="acc", bufs=4)
                 mx(acc[:], wm_q, slice(a * P, (a + 1) * P), ms_q, True, True)
                 nc.scalar.copy(memories[a][:, half * BANK : (half + 1) * BANK], acc[:])
-
-        note_picked = buffer("note_picked", [P, PACK, I], BF16)
-        for t in range(PACK):
-            gather = nc.vector.tensor_copy if t < PACK - 1 else scalar_gather
-            gather(note_picked[:, t, :], note_planes[t][:].indirect(note_list[:]))
-
-        def weave_quantize(name, picked, reuse):
-            woven = buffer(name + "_woven", [P, I, PACK], BF16, reuse)
-            weave(nc.vector.tensor_copy, woven[:], picked[:])
-            return quantize(name, woven[:], I)
 
         def look_up(first, gather, reuse):
             picked = buffer("picked_memories" + str(first), [P, 2, Q], F32, reuse)
@@ -132,31 +130,34 @@ def tile_attend_threesources_memorylarger_lean_kernel(
                 gather(picked[:, a, :], memories[first + a][:].indirect(memory_list[:]))
             return picked
 
-        picked_words = buffer("picked_words", [P, I], U32)
-        nc.vector.tensor_copy(picked_words[:], key_words[:].bitcast(U32).indirect(token_list[:]))
-        note_q = weave_quantize("note", note_picked, "key_words")
-        picked_scales = buffer("picked_scales", [P, I], U8, "key_words")
-        nc.vector.tensor_copy(picked_scales[:], key_scales[:].indirect(token_list[:]))
-        key_q = (picked_words, picked_scales)
-
-
         def gather_in_halves(dst, window, offsets):
             cols = I // 2 // GROUP
             scalar_gather(dst[:, : I // 2], window.indirect(offsets[:, :cols]))
             nc.vector.tensor_copy(dst[:, I // 2 :], window.indirect(offsets[:, cols:]))
 
-        page_picked = buffer("page_picked", [P, PACK, I], BF16)
-        for t in range(PACK - 1):
-            scalar_gather(page_picked[:, t, :], page_planes[t][:].indirect(page_list[:]))
-        gather_in_halves(page_picked[:, PACK - 1, :], page_planes[PACK - 1][:], page_list)
-        page_q = weave_quantize("page", page_picked, None)
-
-        q_q = []
-        for n, copy in enumerate((nc.scalar.copy, nc.scalar.copy, nc.vector.tensor_copy)):
+        def query_operand(n, copy):
             woven = buffer("q_woven" + str(n), [P, Q, PACK], BF16)
             weave(copy, woven[:], q_raw[n][:])
-            q_q.append(quantize("q" + str(n), woven[:], Q))
+            return quantize("q" + str(n), woven[:], Q)
 
+        for t in range(1, PACK):
+            gather_plane(note_picked, note_planes, note_list, t, vector_gather)
+        picked_words = buffer("picked_words", [P, I], U32)
+        vector_gather(picked_words[:], key_words[:].bitcast(U32).indirect(token_list[:]))
+        note_woven = buffer("note_woven", [P, I, PACK], BF16, "key_words")
+        weave(nc.vector.tensor_copy, note_woven[:], note_picked[:])
+        note_q = quantize("note", note_woven[:], I)
+        picked_scales = buffer("picked_scales", [P, I], U8, "key_words")
+        vector_gather(picked_scales[:], key_scales[:].indirect(token_list[:]))
+        key_q = (picked_words, picked_scales)
+        page_picked = buffer("page_picked", [P, PACK, I], F32)
+        for t, gather in enumerate((scalar_gather, scalar_gather, vector_gather, scalar_gather)):
+            gather_plane(page_picked, page_planes, page_list, t, gather)
+        page_woven = buffer("page_woven", [P, I, PACK], BF16)
+        weave(nc.vector.tensor_copy, page_woven[:], page_picked[:])
+        q_q = [query_operand(0, nc.scalar.copy)]
+        page_q = quantize("page", page_woven[:], I, "q_woven0")
+        q_q.extend([query_operand(1, nc.scalar.copy), query_operand(2, nc.vector.tensor_copy)])
         low_memories = look_up(0, scalar_gather, "q_raw1")
 
         scores = [ps.tile([P, I], F32, name="scores" + str(h), tag="score", bufs=2) for h in range(Q // P)]
@@ -182,51 +183,61 @@ def tile_attend_threesources_memorylarger_lean_kernel(
         nc.vector.tensor_copy(picked_vals[0][:], val_rows[0][:].indirect(token_list[:]))
         turn(low_turned[:, 0], picked_vals[0])
         high_memories = look_up(2, nc.vector.tensor_copy, "val_rows0")
-        w_woven = buffer("w_woven", [P, Q, PACK], BF16, "memories3")
+        scalar_gather(picked_vals[1][:], val_rows[1][:].indirect(token_list[:]))
+        gather_in_halves(picked_vals[2][:], val_rows[2][:], token_list)
+        late_woven = buffer("late_woven", [P, 3 * P, PACK], BF16, "val_rows2")
+        w_woven = [buffer("w_woven", [P, P, PACK], BF16, "memories3")[:], late_woven[:, :P, :]]
+        w_q = (buffer("w_codes", [P, Q], U32), buffer("w_scales", [P, Q], U8))
         for h in range(Q // P):
             turned = ps.tile([P, PACK, P], F32, name="w_turned", tag="score", bufs=2)
             for t in range(PACK):
                 nc.tensor.transpose(turned[:, t, :], sig[h][:, t, :], ident[:])
             nc.vector.tensor_tensor(
-                w_woven[:, h * P : (h + 1) * P, :], turned[:].rearrange("p t q -> p q t"),
+                w_woven[h], turned[:].rearrange("p t q -> p q t"),
                 factor[:].unsqueeze(1).to_broadcast([P, P, PACK]), MULT,
             )
-        w_q = quantize("w", w_woven[:], Q)
+        for h in range(Q // P):
+            cols = slice(h * P, (h + 1) * P)
+            nc.vector.quantize_mx(
+                w_q[0][:, cols].bitcast(FP8X4), w_q[1][:, cols], w_woven[h].rearrange("p w t -> p (w t)")
+            )
 
-        scalar_gather(picked_vals[1][:], val_rows[1][:].indirect(token_list[:]))
         turn(low_turned[:, 1], picked_vals[1])
-        scalar_gather(picked_vals[2][:], val_rows[2][:].indirect(token_list[:]))
         turned2 = ps.tile([P, 2, P], F32, name="turned2", tag="turn_b")
         turn(turned2, picked_vals[2])
 
-        low_woven = buffer("low_woven", [P, 2 * P, PACK], BF16, "val_rows2")
+        low_woven = late_woven[:, P:, :]
         nc.scalar.copy(
-            low_woven[:].bitcast(F32).rearrange("p (a e) u -> p a e u", a=2),
+            low_woven.bitcast(F32).rearrange("p (a e) u -> p a e u", a=2),
             low_turned[:].rearrange("p a u e -> p a e u"),
         )
-        low_q = quantize("low_vals", low_woven[:], 2 * P)
+        low_q = quantize("low_vals", low_woven, 2 * P)
         low_acc = ps.tile([P, 2, Q], F32, name="low_acc", tag="acc", bufs=4)
         for a in range(2):
             mx(low_acc[:, a, :], low_q, slice(a * P, (a + 1) * P), w_q, True, True)
 
-        gather_in_halves(picked_vals[3][:], val_rows[3][:], token_list)
-        turned3 = ps.tile([P, 2, P], F32, name="turned3", tag="turn_a")
-        turn(turned3, picked_vals[3])
+        def unturn(a, turned):
+            woven = buffer("v_woven" + str(a), [P, P, PACK], BF16)
+            nc.scalar.copy(woven[:].bitcast(F32), turned[:].rearrange("p u e -> p e u"))
+            return woven
 
-        def multiply(a, turned, copy, reuse):
-            woven = buffer("v_woven" + str(a), [P, P, PACK], BF16, reuse)
-            copy(woven[:].bitcast(F32), turned[:].rearrange("p u e -> p e u"))
-            v_q = quantize("v" + str(a), woven[:], P)
+        def multiply(a, woven, reuse):
             acc = ps.tile([P, Q], F32, name="high_acc", tag="acc", bufs=4)
-            mx(acc[:], v_q, slice(0, P), w_q, True, True)
+            mx(acc[:], quantize("v" + str(a), woven[:], P, reuse), slice(0, P), w_q, True, True)
             return acc
 
-        acc2 = multiply(2, turned2, nc.vector.tensor_copy, "val_rows3")
-        low_result = buffer("low_result", [P, 2, Q], F32, "val_rows3")
-        nc.vector.tensor_tensor(low_result[:], low_acc[:], low_memories[:], MAX)
-        nc.sync.dma_start(out[: 2 * P, :].rearrange("(a p) q -> p a q", a=2), low_result[:])
-        acc3 = multiply(3, turned3, nc.scalar.copy, None)
-        for a, acc in ((2, acc2), (3, acc3)):
+        def finish(a, acc):
             result = buffer("result" + str(a), [P, Q], F32)
             nc.vector.tensor_tensor(result[:], acc[:], high_memories[:, a - 2, :], MAX)
             nc.sync.dma_start(out[a * P : (a + 1) * P, :], result[:])
+
+        woven2 = unturn(2, turned2)
+        gather_in_halves(picked_vals[3][:], val_rows[3][:], token_list)
+        turned3 = ps.tile([P, 2, P], F32, name="turned3", tag="turn_a")
+        turn(turned3, picked_vals[3])
+        acc2 = multiply(2, woven2, "val_rows3")
+        low_result = buffer("low_result", [P, 2, Q], F32, "v_woven2")
+        nc.vector.tensor_tensor(low_result[:], low_acc[:], low_memories[:], MAX)
+        nc.sync.dma_start(out[: 2 * P, :].rearrange("(a p) q -> p a q", a=2), low_result[:])
+        finish(2, acc2)
+        finish(3, multiply(3, unturn(3, turned3), None))

@@ -75,24 +75,24 @@ def tile_attend_threesources_memorylarger_lean_kernel(
             nc.scalar.activation(dst, src, COPY)
 
         key_scales = buffer("key_scales", [P, T], U8)
-        nc.vector.memset(key_scales[:].bitcast(I32), 0)
+        nc.gpsimd.memset(key_scales[:].bitcast(I32), 0)
         ident = buffer("ident", [P, P], F32)
         make_identity(nc, ident[:])
 
         wm_raw = load_rows("wm_raw", wm)
         token_list = load_list("token_list", offs)
-        note_list = load_list("note_list", offs2)
-        page_list = load_list("page_list", offs3)
-        memory_list = load_list("memory_list", offs4)
-        ms_raw = load_rows("ms_raw", mstore)
-        note_planes = load_planes("note_plane", notes)
-        key_words = buffer("key_words", [P, T], I32)
-        nc.sync.dma_start(key_words[:], keys_words[0].rearrange("p n t -> p (n t)").bitcast(I32))
         for quad in range(4):
             nc.sync.dma_start(
                 key_scales[32 * quad : 32 * quad + 4, :].bitcast(I32),
                 keys_scales[0, 4 * quad : 4 * quad + 4, :].bitcast(I32),
             )
+        ms_raw = load_rows("ms_raw", mstore)
+        note_list = load_list("note_list", offs2)
+        note_planes = load_planes("note_plane", notes)
+        key_words = buffer("key_words", [P, T], I32)
+        nc.sync.dma_start(key_words[:], keys_words[0].rearrange("p n t -> p (n t)").bitcast(I32))
+        page_list = load_list("page_list", offs3)
+        memory_list = load_list("memory_list", offs4)
         page_planes = load_planes("page_plane", pages)
         factor = buffer("factor", [P, PACK], F32)
         nc.sync.dma_start(factor[:], slot_factor.rearrange("o (p t) -> (o p) t", t=PACK))
@@ -111,7 +111,12 @@ def tile_attend_threesources_memorylarger_lean_kernel(
             gather(picked[:, t, :], planes[t].indirect(offsets[:]))
 
         vector_gather = nc.vector.tensor_copy
-        ms_woven = [buffer("ms_woven" + str(half), [P, BANK, PACK], BF16) for half in range(M // BANK)]
+        picked_scales = buffer("picked_scales", [P, I], U8, "wm_woven")
+        vector_gather(picked_scales[:], key_scales[:].indirect(token_list[:]))
+        ms_woven = [
+            buffer("ms_woven" + str(half), [P, BANK, PACK], BF16, reuse)
+            for half, reuse in enumerate(("key_scales", None))
+        ]
         for half, copy in enumerate((nc.vector.tensor_copy, nc.scalar.copy)):
             weave(copy, ms_woven[half][:], ms_raw[:, :, half * BANK : (half + 1) * BANK])
         note_picked = buffer("note_picked", [P, PACK, I], F32)
@@ -147,8 +152,6 @@ def tile_attend_threesources_memorylarger_lean_kernel(
         note_woven = buffer("note_woven", [P, I, PACK], BF16, "key_words")
         weave(nc.vector.tensor_copy, note_woven[:], note_picked[:])
         note_q = quantize("note", note_woven[:], I)
-        picked_scales = buffer("picked_scales", [P, I], U8, "key_words")
-        vector_gather(picked_scales[:], key_scales[:].indirect(token_list[:]))
         key_q = (picked_words, picked_scales)
         page_picked = buffer("page_picked", [P, PACK, I], F32)
         for t, gather in enumerate((scalar_gather, scalar_gather, vector_gather, scalar_gather)):

from contextlib import ExitStack

import concourse.mybir as mybir
from concourse.masks import make_identity

D, T, I, Q, E, U, M, C = 512, 2048, 512, 256, 512, 1024, 1024, 512
FLOPS = 2 * (3 * D * Q * I + I * E * Q + C * E * M)

F32 = mybir.dt.float32
BF16 = mybir.dt.bfloat16
I32 = mybir.dt.int32
U32 = mybir.dt.uint32
U16 = mybir.dt.uint16
U8 = mybir.dt.uint8
FP8X4 = mybir.dt.float8_e4m3fn_x4
COPY = mybir.ActivationFunctionType.Copy
SIGMOID = mybir.ActivationFunctionType.Sigmoid
MULT = mybir.AluOpType.mult
MAX = mybir.AluOpType.max

P = 128
PACK = 4
BANK = 512
GROUP = 16


def weave(copy, dst, src):
    copy(dst.rearrange("p (c i) t -> p c t i", i=4), src.rearrange("p t (c i) -> p c t i", i=4))


def tile_attend_threesources_memorylarger_lean_kernel(
    tc, query, query2, query3, keys_words, keys_scales, notes, pages, slot_factor, vals, wm, mstore,
    offs, offs2, offs3, offs4, out,
):
    nc = tc.nc
    with ExitStack() as ctx:
        lists = ctx.enter_context(tc.tile_pool(name="lists", bufs=1))
        sb = ctx.enter_context(tc.tile_pool(name="sb", bufs=1))
        ps = ctx.enter_context(tc.psum_pool(name="ps", bufs=1))

        def buffer(name, shape, dtype, reuse=None):
            return sb.tile(shape, dtype, name=name, tag=reuse or name, align_bytes=64)

        def quantize(name, woven, width, reuse=None):
            codes = buffer(name + "_codes", [P, width], U32, reuse)
            scales = buffer(name + "_scales", [P, width], U8)
            nc.vector.quantize_mx(codes[:].bitcast(FP8X4), scales[:], woven.rearrange("p w t -> p (w t)"))
            return codes, scales

        def mx(acc, left, cols, right, start, stop):
            nc.tensor.matmul_mx(
                acc, lhsT=left[0][:, cols].bitcast(FP8X4), lhsT_scale=left[1][:, cols],
                rhs=right[0][:].bitcast(FP8X4), rhs_scale=right[1][:], start=start, stop=stop,
            )

        def load_rows(name, src):
            raw = buffer(name, [P, PACK, src.shape[1]], F32)
            nc.sync.dma_start(raw[:], src.rearrange("(p t) w -> p t w", t=PACK))
            return raw

        def load_planes(name, src):
            planes = []
            for pair in range(PACK // 2):
                both = buffer(name + str(pair), [P, 2, src.shape[1]], F32)
                nc.sync.dma_start(both[:], src.rearrange("(p t) w -> p t w", t=PACK)[:, 2 * pair : 2 * pair + 2, :])
                planes.extend([both[:, 0, :], both[:, 1, :]])
            return planes

        def load_list(name, src):
            tile = lists.tile([P, src.shape[1]], U16, name=name)
            nc.sync.dma_start(tile[:], src)
            return tile

        def scalar_gather(dst, src):
            nc.scalar.activation(dst, src, COPY)

        key_scales = buffer("key_scales", [P, T], U8)
        nc.gpsimd.memset(key_scales[:].bitcast(I32), 0)
        ident = buffer("ident", [P, P], F32)
        make_identity(nc, ident[:])

        wm_raw = load_rows("wm_raw", wm)
        token_list = load_list("token_list", offs)
        for quad in range(4):
            nc.sync.dma_start(
                key_scales[32 * quad : 32 * quad + 4, :].bitcast(I32),
                keys_scales[0, 4 * quad : 4 * quad + 4, :].bitcast(I32),
            )
        ms_raw = load_rows("ms_raw", mstore)
        note_list = load_list("note_list", offs2)
        note_planes = load_planes("note_plane", notes)
        key_words = buffer("key_words", [P, T], I32)
        nc.sync.dma_start(key_words[:], keys_words[0].rearrange("p n t -> p (n t)").bitcast(I32))
        page_list = load_list("page_list", offs3)
        memory_list = load_list("memory_list", offs4)
        page_planes = load_planes("page_plane", pages)
        factor = buffer("factor", [P, PACK], F32)
        nc.sync.dma_start(factor[:], slot_factor.rearrange("o (p t) -> (o p) t", t=PACK))
        q_raw = [load_rows("q_raw" + str(n), src) for n, src in enumerate((query2, query, query3))]
        val_rows = []
        for a in range(E // P):
            rows = buffer("val_rows" + str(a), [P, T], F32)
            nc.sync.dma_start(rows[:], vals[a * P : (a + 1) * P, :])
            val_rows.append(rows)

        wm_woven = buffer("wm_woven", [P, E, PACK], BF16)
        weave(nc.vector.tensor_copy, wm_woven[:], wm_raw[:])
        wm_q = quantize("wm", wm_woven[:], E)

        def gather_plane(picked, planes, offsets, t, gather):
            gather(picked[:, t, :], planes[t].indirect(offsets[:]))

        vector_gather = nc.vector.tensor_copy
        picked_scales = buffer("picked_scales", [P, I], U8, "wm_woven")
        vector_gather(picked_scales[:], key_scales[:].indirect(token_list[:]))
        ms_woven = [
            buffer("ms_woven" + str(half), [P, BANK, PACK], BF16, reuse)
            for half, reuse in enumerate(("key_scales", None))
        ]
        for half, copy in enumerate((nc.vector.tensor_copy, nc.scalar.copy)):
            weave(copy, ms_woven[half][:], ms_raw[:, :, half * BANK : (half + 1) * BANK])
        note_picked = buffer("note_picked", [P, PACK, I], F32)
        gather_plane(note_picked, note_planes, note_list, 0, scalar_gather)
        memories = [buffer("memories" + str(a), [P, M], F32) for a in range(E // P)]
        for half in range(M // BANK):
            ms_q = quantize("ms" + str(half), ms_woven[half][:], BANK)
            for a in range(E // P):
                acc = ps.tile([P, BANK], F32, name="me_acc", tag="acc", bufs=4)
                mx(acc[:], wm_q, slice(a * P, (a + 1) * P), ms_q, True, True)
                nc.scalar.copy(memories[a][:, half * BANK : (half + 1) * BANK], acc[:])

        def look_up(first, gather, reuse):
            picked = buffer("picked_memories" + str(first), [P, 2, Q], F32, reuse)
            for a in range(2):
                gather(picked[:, a, :], memories[first + a][:].indirect(memory_list[:]))
            return picked

        def gather_in_halves(dst, window, offsets):
            cols = I // 2 // GROUP
            scalar_gather(dst[:, : I // 2], window.indirect(offsets[:, :cols]))
            nc.vector.tensor_copy(dst[:, I // 2 :], window.indirect(offsets[:, cols:]))

        def query_operand(n, copy):
            woven = buffer("q_woven" + str(n), [P, Q, PACK], BF16)
            weave(copy, woven[:], q_raw[n][:])
            return quantize("q" + str(n), woven[:], Q)

        for t in range(1, PACK):
            gather_plane(note_picked, note_planes, note_list, t, vector_gather)
        picked_words = buffer("picked_words", [P, I], U32)
        vector_gather(picked_words[:], key_words[:].bitcast(U32).indirect(token_list[:]))
        note_woven = buffer("note_woven", [P, I, PACK], BF16, "key_words")
        weave(nc.vector.tensor_copy, note_woven[:], note_picked[:])
        note_q = quantize("note", note_woven[:], I)
        key_q = (picked_words, picked_scales)
        page_picked = buffer("page_picked", [P, PACK, I], F32)
        for t, gather in enumerate((scalar_gather, scalar_gather, vector_gather, scalar_gather)):
            gather_plane(page_picked, page_planes, page_list, t, gather)
        page_woven = buffer("page_woven", [P, I, PACK], BF16)
        weave(nc.vector.tensor_copy, page_woven[:], page_picked[:])
        q_q = [query_operand(0, nc.scalar.copy)]
        page_q = quantize("page", page_woven[:], I, "q_woven0")
        q_q.extend([query_operand(1, nc.scalar.copy), query_operand(2, nc.vector.tensor_copy)])
        low_memories = look_up(0, scalar_gather, "q_raw1")

        scores = [ps.tile([P, I], F32, name="scores" + str(h), tag="score", bufs=2) for h in range(Q // P)]
        for n, keys in enumerate((note_q, key_q, page_q)):
            for h in range(Q // P):
                mx(scores[h][:], q_q[n], slice(h * P, (h + 1) * P), keys, n == 0, n == 2)
        sig = []
        for h in range(Q // P):
            dealt = buffer("sig" + str(h), [P, PACK, P], F32)
            nc.scalar.activation(dealt[:], scores[h][:].rearrange("p (s t) -> p t s", t=PACK), SIGMOID)
            sig.append(dealt)

        def turn(bank, picked):
            words = picked[:].bitcast(F32)
            for u in range(2):
                nc.tensor.transpose(bank[:, u, :], words[:, u::2], ident[:])

        picked_vals = [
            buffer("picked_vals" + str(a), [P, I], BF16, reuse)
            for a, reuse in enumerate(("q_woven2", "q2_codes", None, None))
        ]
        low_turned = ps.tile([P, 2, 2, P], F32, name="low_turned", tag="turn_a")
        nc.vector.tensor_copy(picked_vals[0][:], val_rows[0][:].indirect(token_list[:]))
        turn(low_turned[:, 0], picked_vals[0])
        high_memories = look_up(2, nc.vector.tensor_copy, "val_rows0")
        scalar_gather(picked_vals[1][:], val_rows[1][:].indirect(token_list[:]))
        gather_in_halves(picked_vals[2][:], val_rows[2][:], token_list)
        late_woven = buffer("late_woven", [P, 3 * P, PACK], BF16, "val_rows2")
        w_woven = [buffer("w_woven", [P, P, PACK], BF16, "memories3")[:], late_woven[:, :P, :]]
        w_q = (buffer("w_codes", [P, Q], U32), buffer("w_scales", [P, Q], U8))
        for h in range(Q // P):
            turned = ps.tile([P, PACK, P], F32, name="w_turned", tag="score", bufs=2)
            for t in range(PACK):
                nc.tensor.transpose(turned[:, t, :], sig[h][:, t, :], ident[:])
            nc.vector.tensor_tensor(
                w_woven[h], turned[:].rearrange("p t q -> p q t"),
                factor[:].unsqueeze(1).to_broadcast([P, P, PACK]), MULT,
            )
        for h in range(Q // P):
            cols = slice(h * P, (h + 1) * P)
            nc.vector.quantize_mx(
                w_q[0][:, cols].bitcast(FP8X4), w_q[1][:, cols], w_woven[h].rearrange("p w t -> p (w t)")
            )

        turn(low_turned[:, 1], picked_vals[1])
        turned2 = ps.tile([P, 2, P], F32, name="turned2", tag="turn_b")
        turn(turned2, picked_vals[2])

        low_woven = late_woven[:, P:, :]
        nc.scalar.copy(
            low_woven.bitcast(F32).rearrange("p (a e) u -> p a e u", a=2),
            low_turned[:].rearrange("p a u e -> p a e u"),
        )
        low_q = quantize("low_vals", low_woven, 2 * P)
        low_acc = ps.tile([P, 2, Q], F32, name="low_acc", tag="acc", bufs=4)
        for a in range(2):
            mx(low_acc[:, a, :], low_q, slice(a * P, (a + 1) * P), w_q, True, True)

        def unturn(a, turned):
            woven = buffer("v_woven" + str(a), [P, P, PACK], BF16)
            nc.scalar.copy(woven[:].bitcast(F32), turned[:].rearrange("p u e -> p e u"))
            return woven

        def multiply(a, woven, reuse):
            acc = ps.tile([P, Q], F32, name="high_acc", tag="acc", bufs=4)
            mx(acc[:], quantize("v" + str(a), woven[:], P, reuse), slice(0, P), w_q, True, True)
            return acc

        def finish(a, acc):
            result = buffer("result" + str(a), [P, Q], F32)
            nc.vector.tensor_tensor(result[:], acc[:], high_memories[:, a - 2, :], MAX)
            nc.sync.dma_start(out[a * P : (a + 1) * P, :], result[:])

        woven2 = unturn(2, turned2)
        gather_in_halves(picked_vals[3][:], val_rows[3][:], token_list)
        turned3 = ps.tile([P, 2, P], F32, name="turned3", tag="turn_a")
        turn(turned3, picked_vals[3])
        acc2 = multiply(2, woven2, "val_rows3")
        low_result = buffer("low_result", [P, 2, Q], F32, "v_woven2")
        nc.vector.tensor_tensor(low_result[:], low_acc[:], low_memories[:], MAX)
        nc.sync.dma_start(out[: 2 * P, :].rearrange("(a p) q -> p a q", a=2), low_result[:])
        finish(2, acc2)
        finish(3, multiply(3, unturn(3, turned3), None))
